import numpy as np
import ml_dtypes


def mxq(x, axis, fmt="e4m3"):
    dtype, down = {"e4m3": (ml_dtypes.float8_e4m3fn, 7), "e5m2": (ml_dtypes.float8_e5m2, 14)}[fmt]
    v = np.moveaxis(np.asarray(x, np.float32).astype(ml_dtypes.bfloat16).astype(np.float64), axis, -1)
    blocks = v.reshape(v.shape[:-1] + (-1, 32))
    amax = np.abs(blocks).max(-1, keepdims=True)
    byte = np.maximum(np.where(amax > 0, np.frexp(amax)[1] - 1 + 127, 0) - down, 1)
    scale = np.exp2(byte - 127.0)
    codes = (blocks / scale).astype(np.float32).astype(dtype).astype(np.float64)
    return np.moveaxis((codes * scale).reshape(v.shape), -1, axis)


WIDE = False


def mx_kscale(k):
    if not WIDE:
        return np.ones(k)
    levels = np.array([10, -10, 5, -5, 0])
    if k % 512:
        return np.exp2(np.random.permutation(np.resize(levels, k // 32))).repeat(32)
    a = np.empty((k // 512, 16))
    for p in range(k // 512):
        a[p, :8] = np.random.permutation(np.resize(levels, 8))
        for g in range(8):
            far = levels[np.abs(levels - a[p, g]) >= 10]
            a[p, g + 8] = far[np.random.randint(len(far))]
    return np.exp2(a.ravel()).repeat(32)


BF16 = ml_dtypes.bfloat16


def bf(x):
    return np.asarray(x, np.float32).astype(BF16)


def f64(x):
    return np.asarray(x).astype(np.float64)

E4M3FN = np.array([(-1.0 if i & 128 else 1.0) * ((1.0 + (i & 7) / 8.0) * 2.0 ** (((i >> 3) & 15) - 7) if i & 120 else (i & 7) * 2.0 ** -9) for i in range(256)])


def e4m3fn_bytes(y):
    return np.clip(np.asarray(y, np.float64), -448.0, 448.0).astype(np.float32).astype(ml_dtypes.float8_e4m3fn).view(np.uint8)


def e4m3fn_values(b):
    return E4M3FN[b]


T, K, D, N, G = 1536, 2048, 1024, 512, 128


def setup_inputs():
    s, t = mx_kscale(K), mx_kscale(D)
    X = np.random.standard_normal((T, K)) * s
    R = np.random.standard_normal((N, D)) / t
    X_scale = (np.abs(X).reshape(T, K // G, G).max(axis=2) / 448.0).astype(np.float32)
    R_scale = (np.abs(R).reshape(N // G, G, D // G, G).max(axis=(1, 3)) / 448.0).astype(np.float32)
    return {"X_bytes": e4m3fn_bytes(X / np.repeat(f64(X_scale), G, axis=1)),
            "X_scale": X_scale,
            "B": bf(np.random.standard_normal((K, N)) / np.sqrt(K) / s[:, None]),
            "Q": bf(np.random.standard_normal((T, D)) * t),
            "v": bf(0.3 * np.random.standard_normal(D) * t),
            "R_bytes": e4m3fn_bytes(R / np.repeat(np.repeat(f64(R_scale), G, axis=0), G, axis=1)),
            "R_scale": R_scale,
            "g": bf(1.0 + 0.1 * np.random.standard_normal(N))}


def reference(X_bytes, X_scale, B, Q, v, R_bytes, R_scale, g):
    X = e4m3fn_values(X_bytes) * np.repeat(f64(X_scale), G, axis=1)
    R = e4m3fn_values(R_bytes) * np.repeat(np.repeat(f64(R_scale), G, axis=0), G, axis=1)
    C = f64(Q) + f64(v)
    pos = mxq(C, 1, "e4m3") @ mxq(R, 1, "e4m3").T
    bias = mxq(X, 1, "e4m3") @ mxq(f64(B), 0, "e4m3")
    return (pos / np.sqrt(D) + bias) * f64(g)

@@ -1,0 +1,249 @@
+from contextlib import ExitStack
+
+import concourse.mybir as mybir
+from concourse.masks import make_identity
+
+T, K, D, N, G = 1536, 2048, 1024, 512, 128
+P = 128
+NT = T // P
+KP = K // 512
+DP = D // 512
+NB = K // G
+RB = D // G
+RT = N // P
+S_BLOCKS = 8
+
+FLOPS = 2 * T * N * (K + D)
+
+F32 = mybir.dt.float32
+BF16 = mybir.dt.bfloat16
+U32 = mybir.dt.uint32
+U8 = mybir.dt.uint8
+FP8 = mybir.dt.float8_e4m3fn
+FP8X4 = mybir.dt.float8_e4m3fn_x4
+MULT = mybir.AluOpType.mult
+ADD = mybir.AluOpType.add
+COPY = mybir.ActivationFunctionType.Copy
+
+
+def tile_relative_offset_scores_d9_kernel(tc, X_bytes, X_scale, B, Q, v, R_bytes, R_scale, g, out):
+    nc = tc.nc
+    with ExitStack() as ctx:
+        keep = ctx.enter_context(tc.tile_pool(name="keep", bufs=1))
+        work = ctx.enter_context(tc.tile_pool(name="work", bufs=3))
+        psum = ctx.enter_context(tc.psum_pool(name="psum", bufs=2))
+
+        vg = keep.tile([P, D + N], BF16, align_bytes=64)
+        nc.gpsimd.memset(vg[:], 0.0)
+        ones = keep.tile([P, P], BF16, align_bytes=64)
+        nc.vector.memset(ones[:], 1.0)
+        ident = keep.tile([P, P], F32, align_bytes=64)
+        make_identity(nc, ident[:])
+
+        xs = keep.tile([P, NT * NB], F32, align_bytes=64)
+        rs = keep.tile([P, RT * RB], F32, align_bytes=64)
+        rs32 = keep.tile([P, RT * RB], F32, align_bytes=64)
+        rb = keep.tile([P, RT, D], U8, align_bytes=64)
+        xb = [keep.tile([P, K], U8, name=f"xb{i}", align_bytes=64) for i in range(NT)]
+        qb = [keep.tile([P, D], BF16, name=f"qb{i}", align_bytes=64) for i in range(NT)]
+        br = [keep.tile([P, 4, N], BF16, name=f"br{c}", align_bytes=64) for c in range(KP)]
+        X_v = X_bytes.rearrange("(p i) k -> p i k", i=NT)
+        Q_v = Q.rearrange("(p i) k -> p i k", i=NT)
+        B_v = B.rearrange("(c p j) n -> c p j n", p=P, j=4)
+        O_v = out.rearrange("(p i) n -> p i n", i=NT)
+
+        def load_x(i):
+            nc.sync.dma_start(out=xb[i][:], in_=X_v[:, i, :])
+
+        def load_q(i):
+            nc.sync.dma_start(out=qb[i][:], in_=Q_v[:, i, :])
+
+        def load_b(c):
+            nc.sync.dma_start(out=br[c][:], in_=B_v[c])
+
+        nc.scalar.dma_start(out=rs[:], in_=R_scale.rearrange("a b -> (a b)").partition_broadcast(P))
+        nc.scalar.dma_start(out=vg[0:1, 0:D], in_=v.rearrange("(o k) -> o k", o=1))
+        nc.scalar.dma_start(out=vg[0:1, D : D + N], in_=g.rearrange("(o k) -> o k", o=1))
+        nc.sync.dma_start(out=xs[:], in_=X_scale.rearrange("(p i) j -> p (i j)", i=NT))
+        load_x(0)
+        nc.sync.dma_start(out=rb[:], in_=R_bytes.rearrange("(c r) k -> r c k", r=P))
+        load_q(0)
+        load_b(0)
+        load_x(1)
+        load_b(1)
+        load_q(1)
+        load_b(2)
+        load_x(2)
+        load_b(3)
+        load_q(2)
+        for i in range(3, NT):
+            load_x(i)
+            load_q(i)
+
+        vbc = keep.tile([P, D], BF16, align_bytes=64)
+        gbc = keep.tile([P, N], F32, align_bytes=64)
+        banks = []
+        for h, tag in enumerate(("x01", "x23", "q")):
+            bank = psum.tile([P, 512], F32, name=f"bc{h}", tag=tag)
+            nc.tensor.matmul(bank[:], lhsT=ones[:], rhs=vg[:, 512 * h : 512 * h + 512], start=True, stop=True)
+            banks.append(bank)
+        vbc_v = vbc[:].rearrange("r (u g p e) -> r g u p e", u=2, g=DP, e=2)
+        for h in range(DP):
+            nc.scalar.copy(out=vbc_v[:, h], in_=banks[h][:].rearrange("r (p u e) -> r u p e", u=2, e=2))
+        nc.scalar.copy(out=gbc[:], in_=banks[2][:])
+        nc.vector.tensor_scalar(out=rs32[:], in0=rs[:], scalar1=1.0 / 32.0, scalar2=None, op0=MULT)
+
+        rw = keep.tile([P, RT, D], BF16, align_bytes=64)
+        rg = keep.tile([P, DP, N, 4], BF16, align_bytes=64)
+        rc = keep.tile([P, DP, N], U32, align_bytes=64)
+        rsc = keep.tile([P, DP, N], U8, align_bytes=64)
+
+        def widen_block(out_tile, in_ap, scale, blk):
+            c, q = blk // 4, blk % 4
+            dst = out_tile.rearrange("r (c u p e) -> r c p u e", u=2, p=P, e=2)
+            nc.vector.tensor_scalar(
+                out=dst[:, c, 32 * q : 32 * q + 32],
+                in0=in_ap[:, G * blk : G * blk + G].bitcast(FP8).rearrange("r (p u e) -> r p u e", u=2, e=2),
+                scalar1=scale, scalar2=None, op0=MULT)
+
+        def r_widen(t):
+            for blk in range(RB):
+                widen_block(rw[:, t, :], rb[:, t, :], rs32[:, RB * t + blk : RB * t + blk + 1], blk)
+
+        def r_turn(t):
+            bank = psum.tile([P, DP, 2, P], F32, name="rbank", tag=("x01", "x23", "q", "x01")[t])
+            words = rw[:, t, :].bitcast(F32)
+            for c in range(DP):
+                for u in range(2):
+                    w = 256 * c + 128 * u
+                    nc.tensor.transpose(bank[:, c, u, :], words[:, w : w + P], ident[:])
+            dst = rg[:].rearrange("p c n t -> p (c n t)").bitcast(F32).rearrange("p (c n u) -> p c n u", c=DP, u=2)
+            nc.scalar.copy(out=dst[:, :, P * t : P * t + P, :], in_=bank[:].rearrange("p c u r -> p c r u"))
+
+        def r_quant(c):
+            nc.vector.quantize_mx(out=rc[:, c, :].bitcast(FP8X4), scales=rsc[:, c, :],
+                                  in_=rg[:, c].rearrange("p n t -> p (n t)"))
+
+        bg = [keep.tile([P, N, 4], BF16, name=f"bg{c}", align_bytes=64) for c in range(KP)]
+        bc = keep.tile([P, KP, N], U32, align_bytes=64)
+        bsc = keep.tile([P, KP, N], U8, align_bytes=64)
+
+        def b_group(c):
+            nc.vector.tensor_copy(out=bg[c][:], in_=br[c][:].rearrange("p j n -> p n j"))
+
+        def b_quant(c):
+            nc.vector.quantize_mx(out=bc[:, c, :].bitcast(FP8X4), scales=bsc[:, c, :],
+                                  in_=bg[c][:].rearrange("p n t -> p (n t)"))
+
+        st = {}
+
+        def widen(i):
+            xw = work.tile([P, K], BF16, align_bytes=64)
+            for blk in range(S_BLOCKS):
+                nc.scalar.activation(out=xw[:, G * blk : G * blk + G],
+                                     in_=xb[i][:, G * blk : G * blk + G].bitcast(FP8),
+                                     func=COPY, scale=xs[:, NB * i + blk : NB * i + blk + 1])
+            for blk in range(S_BLOCKS, NB):
+                widen_block(xw[:], xb[i][:], xs[:, NB * i + blk : NB * i + blk + 1], blk)
+            st["xw", i] = xw
+
+        def add(i):
+            cw = work.tile([P, D], BF16, align_bytes=64)
+            nc.vector.tensor_tensor(
+                out=cw[:].rearrange("r (u w e) -> r u w e", u=2, e=2),
+                in0=qb[i][:].rearrange("r (w u e) -> r u w e", u=2, e=2),
+                in1=vbc[:].rearrange("r (u w e) -> r u w e", u=2, e=2), op=ADD)
+            st["cw", i] = cw
+
+        def turn(i):
+            xw = st.pop(("xw", i))
+            cw = st.pop(("cw", i))
+            words = xw[:].bitcast(F32)
+            cwords = cw[:].bitcast(F32)
+            xg = work.tile([P, KP, P, 4], BF16, align_bytes=64)
+            cg = work.tile([P, DP, P, 4], BF16, align_bytes=64)
+            xgw = xg[:].rearrange("p c r t -> p (c r t)").bitcast(F32).rearrange("p (c r u) -> p c r u", c=KP, u=2)
+            cgw = cg[:].rearrange("p c r t -> p (c r t)").bitcast(F32).rearrange("p (c r u) -> p c r u", c=DP, u=2)
+            for h, tag in enumerate(("x01", "x23")):
+                bank = psum.tile([P, 2, 2, P], F32, name="xbank", tag=tag)
+                for cc in range(2):
+                    c = 2 * h + cc
+                    for u in range(2):
+                        if 4 * c < S_BLOCKS:
+                            src = words[:, 256 * c + u : 256 * (c + 1) : 2]
+                        else:
+                            src = words[:, 256 * c + P * u : 256 * c + P * u + P]
+                        nc.tensor.transpose(bank[:, cc, u, :], src, ident[:])
+                nc.scalar.copy(out=xgw[:, 2 * h : 2 * h + 2], in_=bank[:].rearrange("p c u r -> p c r u"))
+            bank = psum.tile([P, 2, 2, P], F32, name="qbank", tag="q")
+            for c in range(DP):
+                for u in range(2):
+                    w = 256 * u + P * c
+                    nc.tensor.transpose(bank[:, c, u, :], cwords[:, w : w + P], ident[:])
+            nc.scalar.copy(out=cgw[:], in_=bank[:].rearrange("p c u r -> p c r u"))
+            st["xg", i] = xg
+            st["cg", i] = cg
+
+        def quant(i):
+            xg = st.pop(("xg", i))
+            cg = st.pop(("cg", i))
+            xc = work.tile([P, KP, P], U32, align_bytes=64)
+            xsc = work.tile([P, KP, P], U8, align_bytes=64)
+            cc = work.tile([P, DP, P], U32, align_bytes=64)
+            csc = work.tile([P, DP, P], U8, align_bytes=64)
+            nc.vector.quantize_mx(out=cc[:].rearrange("p c r -> p (c r)").bitcast(FP8X4),
+                                  scales=csc[:].rearrange("p c r -> p (c r)"),
+                                  in_=cg[:].rearrange("p c r t -> p (c r t)"))
+            nc.vector.quantize_mx(out=xc[:].rearrange("p c r -> p (c r)").bitcast(FP8X4),
+                                  scales=xsc[:].rearrange("p c r -> p (c r)"),
+                                  in_=xg[:].rearrange("p c r t -> p (c r t)"))
+            st["code", i] = (xc, xsc, cc, csc)
+
+        def multiply(i):
+            xc, xsc, cc, csc = st.pop(("code", i))
+            acc = psum.tile([P, N], F32)
+            for c in range(DP):
+                nc.tensor.matmul_mx(out=acc[:], lhsT=cc[:, c, :].bitcast(FP8X4), lhsT_scale=csc[:, c, :],
+                                    rhs=rc[:, c, :].bitcast(FP8X4), rhs_scale=rsc[:, c, :],
+                                    start=(c == 0), stop=False)
+            for c in range(KP):
+                nc.tensor.matmul_mx(out=acc[:], lhsT=xc[:, c, :].bitcast(FP8X4), lhsT_scale=xsc[:, c, :],
+                                    rhs=bc[:, c, :].bitcast(FP8X4), rhs_scale=bsc[:, c, :],
+                                    start=False, stop=(c == KP - 1))
+            st["acc", i] = acc
+
+        def finish(i):
+            acc = st.pop(("acc", i))
+            o = work.tile([P, N], F32, align_bytes=64)
+            nc.vector.tensor_tensor(out=o[:], in0=acc[:], in1=gbc[:], op=MULT)
+            nc.sync.dma_start(out=O_v[:, i, :], in_=o[:])
+
+        for s in range(NT + 3):
+            if s >= 3:
+                finish(s - 3)
+            if 2 <= s < NT + 2:
+                quant(s - 2)
+            if s < NT:
+                widen(s)
+                add(s)
+            if s == 0:
+                for t in range(RT):
+                    r_widen(t)
+            if 1 <= s < NT + 1:
+                turn(s - 1)
+            if s == 0:
+                for t in range(RT):
+                    r_turn(t)
+                b_group(0)
+                for c in range(DP):
+                    r_quant(c)
+                b_group(1)
+                b_quant(0)
+            if s == 1:
+                b_group(2)
+                b_quant(1)
+                b_group(3)
+                b_quant(2)
+                b_quant(3)
+            if 2 <= s < NT + 2:
+                multiply(s - 2)

@@ -12,6 +12,10 @@ NB = K // G
 RB = D // G
 RT = N // P
 S_BLOCKS = 8
+TURN_BANKS = 5
+WORK_BUFS = 5
+S_ROWS = (0, 1)
+ACC_BANKS = 3
 
 FLOPS = 2 * T * N * (K + D)
 
@@ -30,11 +34,11 @@ def tile_relative_offset_scores_d9_kernel(tc, X_bytes, X_scale, B, Q, v, R_bytes
     nc = tc.nc
     with ExitStack() as ctx:
         keep = ctx.enter_context(tc.tile_pool(name="keep", bufs=1))
-        work = ctx.enter_context(tc.tile_pool(name="work", bufs=3))
-        psum = ctx.enter_context(tc.psum_pool(name="psum", bufs=2))
+        work = ctx.enter_context(tc.tile_pool(name="work", bufs=WORK_BUFS))
+        psum = ctx.enter_context(tc.psum_pool(name="psum", bufs=TURN_BANKS))
 
-        vg = keep.tile([P, D + N], BF16, align_bytes=64)
-        nc.gpsimd.memset(vg[:], 0.0)
+        vrow = keep.tile([P, D], BF16, align_bytes=64)
+        nc.gpsimd.memset(vrow[:], 0.0)
         ones = keep.tile([P, P], BF16, align_bytes=64)
         nc.vector.memset(ones[:], 1.0)
         ident = keep.tile([P, P], F32, align_bytes=64)
@@ -43,7 +47,7 @@ def tile_relative_offset_scores_d9_kernel(tc, X_bytes, X_scale, B, Q, v, R_bytes
         xs = keep.tile([P, NT * NB], F32, align_bytes=64)
         rs = keep.tile([P, RT * RB], F32, align_bytes=64)
         rs32 = keep.tile([P, RT * RB], F32, align_bytes=64)
-        rb = keep.tile([P, RT, D], U8, align_bytes=64)
+        rb = [keep.tile([P, D], U8, name=f"rb{t}", align_bytes=64) for t in range(RT)]
         xb = [keep.tile([P, K], U8, name=f"xb{i}", align_bytes=64) for i in range(NT)]
         qb = [keep.tile([P, D], BF16, name=f"qb{i}", align_bytes=64) for i in range(NT)]
         br = [keep.tile([P, 4, N], BF16, name=f"br{c}", align_bytes=64) for c in range(KP)]
@@ -58,15 +62,20 @@ def tile_relative_offset_scores_d9_kernel(tc, X_bytes, X_scale, B, Q, v, R_bytes
         def load_q(i):
             nc.sync.dma_start(out=qb[i][:], in_=Q_v[:, i, :])
 
+        def load_r(t):
+            nc.sync.dma_start(out=rb[t][:], in_=R_bytes[P * t : P * t + P, :])
+
         def load_b(c):
             nc.sync.dma_start(out=br[c][:], in_=B_v[c])
 
         nc.scalar.dma_start(out=rs[:], in_=R_scale.rearrange("a b -> (a b)").partition_broadcast(P))
-        nc.scalar.dma_start(out=vg[0:1, 0:D], in_=v.rearrange("(o k) -> o k", o=1))
-        nc.scalar.dma_start(out=vg[0:1, D : D + N], in_=g.rearrange("(o k) -> o k", o=1))
+        nc.scalar.dma_start(out=vrow[0:1, :], in_=v.rearrange("(o k) -> o k", o=1))
         nc.sync.dma_start(out=xs[:], in_=X_scale.rearrange("(p i) j -> p (i j)", i=NT))
         load_x(0)
-        nc.sync.dma_start(out=rb[:], in_=R_bytes.rearrange("(c r) k -> r c k", r=P))
+        load_r(0)
+        load_r(1)
+        load_r(2)
+        load_r(3)
         load_q(0)
         load_b(0)
         load_x(1)
@@ -76,29 +85,55 @@ def tile_relative_offset_scores_d9_kernel(tc, X_bytes, X_scale, B, Q, v, R_bytes
         load_x(2)
         load_b(3)
         load_q(2)
-        for i in range(3, NT):
-            load_x(i)
-            load_q(i)
+        load_x(3)
+        load_q(3)
+        load_x(4)
+        gbc = keep.tile([P, N], BF16, align_bytes=64)
+        nc.sync.dma_start(out=gbc[:], in_=g.partition_broadcast(P))
+        load_q(4)
+        load_x(5)
+        load_q(5)
+        load_x(6)
+        load_q(6)
+        load_x(7)
+        load_q(7)
+        load_x(8)
+        load_q(8)
+        load_x(9)
+        load_q(9)
+        load_x(10)
+        load_q(10)
+        load_x(11)
+        load_q(11)
+        ctx.enter_context(tc.manual_schedule())
 
         vbc = keep.tile([P, D], BF16, align_bytes=64)
-        gbc = keep.tile([P, N], F32, align_bytes=64)
-        banks = []
-        for h, tag in enumerate(("x01", "x23", "q")):
-            bank = psum.tile([P, 512], F32, name=f"bc{h}", tag=tag)
-            nc.tensor.matmul(bank[:], lhsT=ones[:], rhs=vg[:, 512 * h : 512 * h + 512], start=True, stop=True)
-            banks.append(bank)
         vbc_v = vbc[:].rearrange("r (u g p e) -> r g u p e", u=2, g=DP, e=2)
-        for h in range(DP):
-            nc.scalar.copy(out=vbc_v[:, h], in_=banks[h][:].rearrange("r (p u e) -> r u p e", u=2, e=2))
-        nc.scalar.copy(out=gbc[:], in_=banks[2][:])
         nc.vector.tensor_scalar(out=rs32[:], in0=rs[:], scalar1=1.0 / 32.0, scalar2=None, op0=MULT)
+        st = {}
 
-        rw = keep.tile([P, RT, D], BF16, align_bytes=64)
+        def turn_bank(key):
+            bank = psum.tile([P, 2, 2, P], F32, name="bank", tag="turn")
+            st[key] = bank
+            return bank
+
+        def bc(h):
+            bank = turn_bank(("bc", h))
+            nc.tensor.matmul(bank[:].rearrange("p c u r -> p (c u r)"), lhsT=ones[:], rhs=vrow[:, 512 * h : 512 * h + 512],
+                             start=True, stop=True)
+
+        def bev(h):
+            bank = st.pop(("bc", h))
+            nc.scalar.copy(out=vbc_v[:, h],
+                           in_=bank[:].rearrange("p c u r -> p (c u r)").rearrange("r (p u e) -> r u p e", u=2, e=2))
+
+        rw_t = keep.tile([P, RT, D], BF16, align_bytes=64)
         rg = keep.tile([P, DP, N, 4], BF16, align_bytes=64)
+        rgw = rg[:].rearrange("p c n t -> p (c n t)").bitcast(F32).rearrange("p (c n u) -> p c n u", c=DP, u=2)
         rc = keep.tile([P, DP, N], U32, align_bytes=64)
         rsc = keep.tile([P, DP, N], U8, align_bytes=64)
 
-        def widen_block(out_tile, in_ap, scale, blk):
+        def v_widen(out_tile, in_ap, scale, blk):
             c, q = blk // 4, blk % 4
             dst = out_tile.rearrange("r (c u p e) -> r c p u e", u=2, p=P, e=2)
             nc.vector.tensor_scalar(
@@ -106,144 +141,174 @@ def tile_relative_offset_scores_d9_kernel(tc, X_bytes, X_scale, B, Q, v, R_bytes
                 in0=in_ap[:, G * blk : G * blk + G].bitcast(FP8).rearrange("r (p u e) -> r p u e", u=2, e=2),
                 scalar1=scale, scalar2=None, op0=MULT)
 
-        def r_widen(t):
+        def s_widen(out_tile, in_ap, scale, blk):
+            nc.scalar.activation(out=out_tile[:, G * blk : G * blk + G],
+                                 in_=in_ap[:, G * blk : G * blk + G].bitcast(FP8), func=COPY, scale=scale)
+
+        def rw(t):
             for blk in range(RB):
-                widen_block(rw[:, t, :], rb[:, t, :], rs32[:, RB * t + blk : RB * t + blk + 1], blk)
+                (s_widen if t in S_ROWS else v_widen)(
+                    rw_t[:, t, :], rb[t][:], rs32[:, RB * t + blk : RB * t + blk + 1], blk)
 
-        def r_turn(t):
-            bank = psum.tile([P, DP, 2, P], F32, name="rbank", tag=("x01", "x23", "q", "x01")[t])
-            words = rw[:, t, :].bitcast(F32)
-            for c in range(DP):
+        def transposes(bank, words, first, natural):
+            for c in range(2):
                 for u in range(2):
-                    w = 256 * c + 128 * u
-                    nc.tensor.transpose(bank[:, c, u, :], words[:, w : w + P], ident[:])
-            dst = rg[:].rearrange("p c n t -> p (c n t)").bitcast(F32).rearrange("p (c n u) -> p c n u", c=DP, u=2)
-            nc.scalar.copy(out=dst[:, :, P * t : P * t + P, :], in_=bank[:].rearrange("p c u r -> p c r u"))
+                    w = 256 * (first + c)
+                    src = words[:, w + u : w + 256 : 2] if natural else words[:, w + P * u : w + P * u + P]
+                    nc.tensor.transpose(bank[:, c, u, :], src, ident[:])
 
-        def r_quant(c):
+        def rt(t):
+            transposes(turn_bank(("rt", t)), rw_t[:, t, :].bitcast(F32), 0, t in S_ROWS)
+
+        def re(t):
+            bank = st.pop(("rt", t))
+            nc.scalar.copy(out=rgw[:, :, P * t : P * t + P, :], in_=bank[:].rearrange("p c u r -> p c r u"))
+
+        def rz(c):
             nc.vector.quantize_mx(out=rc[:, c, :].bitcast(FP8X4), scales=rsc[:, c, :],
                                   in_=rg[:, c].rearrange("p n t -> p (n t)"))
 
-        bg = [keep.tile([P, N, 4], BF16, name=f"bg{c}", align_bytes=64) for c in range(KP)]
-        bc = keep.tile([P, KP, N], U32, align_bytes=64)
-        bsc = keep.tile([P, KP, N], U8, align_bytes=64)
+        b_grp = [keep.tile([P, N, 4], BF16, name=f"bg{c}", align_bytes=64) for c in range(KP)]
+        b_code = keep.tile([P, KP, N], U32, align_bytes=64)
+        b_scale = keep.tile([P, KP, N], U8, align_bytes=64)
 
-        def b_group(c):
-            nc.vector.tensor_copy(out=bg[c][:], in_=br[c][:].rearrange("p j n -> p n j"))
+        def bg(c):
+            nc.vector.tensor_copy(out=b_grp[c][:], in_=br[c][:].rearrange("p j n -> p n j"))
 
-        def b_quant(c):
-            nc.vector.quantize_mx(out=bc[:, c, :].bitcast(FP8X4), scales=bsc[:, c, :],
-                                  in_=bg[c][:].rearrange("p n t -> p (n t)"))
+        def bz(c):
+            nc.vector.quantize_mx(out=b_code[:, c, :].bitcast(FP8X4), scales=b_scale[:, c, :],
+                                  in_=b_grp[c][:].rearrange("p n t -> p (n t)"))
 
-        st = {}
+        xw = [None] * NT
+        cw = [None] * NT
+        xg = [None] * NT
+        cg = [None] * NT
+        codes = [None] * NT
+        acc = [None] * NT
 
-        def widen(i):
-            xw = work.tile([P, K], BF16, align_bytes=64)
+        def xw_tile(i):
+            if xw[i] is None:
+                t = work.tile([P, K], BF16, name="xw", align_bytes=64)
+                xw[i] = t
+
+        def ws(i):
+            xw_tile(i)
             for blk in range(S_BLOCKS):
-                nc.scalar.activation(out=xw[:, G * blk : G * blk + G],
-                                     in_=xb[i][:, G * blk : G * blk + G].bitcast(FP8),
-                                     func=COPY, scale=xs[:, NB * i + blk : NB * i + blk + 1])
-            for blk in range(S_BLOCKS, NB):
-                widen_block(xw[:], xb[i][:], xs[:, NB * i + blk : NB * i + blk + 1], blk)
-            st["xw", i] = xw
+                s_widen(xw[i][:], xb[i][:], xs[:, NB * i + blk : NB * i + blk + 1], blk)
 
-        def add(i):
-            cw = work.tile([P, D], BF16, align_bytes=64)
+        def wv(i):
+            xw_tile(i)
+            for blk in range(S_BLOCKS, NB):
+                v_widen(xw[i][:], xb[i][:], xs[:, NB * i + blk : NB * i + blk + 1], blk)
+
+        def ad(i):
+            t = work.tile([P, D], BF16, name="cw", align_bytes=64)
+            cw[i] = t
             nc.vector.tensor_tensor(
-                out=cw[:].rearrange("r (u w e) -> r u w e", u=2, e=2),
+                out=t[:].rearrange("r (u w e) -> r u w e", u=2, e=2),
                 in0=qb[i][:].rearrange("r (w u e) -> r u w e", u=2, e=2),
                 in1=vbc[:].rearrange("r (u w e) -> r u w e", u=2, e=2), op=ADD)
-            st["cw", i] = cw
 
-        def turn(i):
-            xw = st.pop(("xw", i))
-            cw = st.pop(("cw", i))
-            words = xw[:].bitcast(F32)
-            cwords = cw[:].bitcast(F32)
-            xg = work.tile([P, KP, P, 4], BF16, align_bytes=64)
-            cg = work.tile([P, DP, P, 4], BF16, align_bytes=64)
-            xgw = xg[:].rearrange("p c r t -> p (c r t)").bitcast(F32).rearrange("p (c r u) -> p c r u", c=KP, u=2)
-            cgw = cg[:].rearrange("p c r t -> p (c r t)").bitcast(F32).rearrange("p (c r u) -> p c r u", c=DP, u=2)
-            for h, tag in enumerate(("x01", "x23")):
-                bank = psum.tile([P, 2, 2, P], F32, name="xbank", tag=tag)
-                for cc in range(2):
-                    c = 2 * h + cc
-                    for u in range(2):
-                        if 4 * c < S_BLOCKS:
-                            src = words[:, 256 * c + u : 256 * (c + 1) : 2]
-                        else:
-                            src = words[:, 256 * c + P * u : 256 * c + P * u + P]
-                        nc.tensor.transpose(bank[:, cc, u, :], src, ident[:])
-                nc.scalar.copy(out=xgw[:, 2 * h : 2 * h + 2], in_=bank[:].rearrange("p c u r -> p c r u"))
-            bank = psum.tile([P, 2, 2, P], F32, name="qbank", tag="q")
+        def tx0(i):
+            transposes(turn_bank(("x0", i)), xw[i][:].bitcast(F32), 0, S_BLOCKS >= 8)
+
+        def tx1(i):
+            transposes(turn_bank(("x1", i)), xw[i][:].bitcast(F32), 2, False)
+
+        def xg_words(i):
+            if xg[i] is None:
+                t = work.tile([P, KP, P, 4], BF16, name="xg", align_bytes=64)
+                xg[i] = t
+            return xg[i][:].rearrange("p c r t -> p (c r t)").bitcast(F32).rearrange("p (c r u) -> p c r u", c=KP, u=2)
+
+        def ex0(i):
+            bank = st.pop(("x0", i))
+            nc.scalar.copy(out=xg_words(i)[:, 0:2], in_=bank[:].rearrange("p c u r -> p c r u"))
+
+        def ex1(i):
+            bank = st.pop(("x1", i))
+            nc.scalar.copy(out=xg_words(i)[:, 2:4], in_=bank[:].rearrange("p c u r -> p c r u"))
+
+        def tq(i):
+            bank = turn_bank(("q", i))
+            words = cw[i][:].bitcast(F32)
             for c in range(DP):
                 for u in range(2):
                     w = 256 * u + P * c
-                    nc.tensor.transpose(bank[:, c, u, :], cwords[:, w : w + P], ident[:])
-            nc.scalar.copy(out=cgw[:], in_=bank[:].rearrange("p c u r -> p c r u"))
-            st["xg", i] = xg
-            st["cg", i] = cg
+                    nc.tensor.transpose(bank[:, c, u, :], words[:, w : w + P], ident[:])
 
-        def quant(i):
-            xg = st.pop(("xg", i))
-            cg = st.pop(("cg", i))
+        def eq(i):
+            bank = st.pop(("q", i))
+            t = work.tile([P, DP, P, 4], BF16, name="cg", align_bytes=64)
+            cg[i] = t
+            words = t[:].rearrange("p c r t -> p (c r t)").bitcast(F32).rearrange("p (c r u) -> p c r u", c=DP, u=2)
+            nc.scalar.copy(out=words, in_=bank[:].rearrange("p c u r -> p c r u"))
+
+        def zx(i):
             xc = work.tile([P, KP, P], U32, align_bytes=64)
             xsc = work.tile([P, KP, P], U8, align_bytes=64)
+            nc.vector.quantize_mx(out=xc[:].rearrange("p c r -> p (c r)").bitcast(FP8X4),
+                                  scales=xsc[:].rearrange("p c r -> p (c r)"),
+                                  in_=xg[i][:].rearrange("p c r t -> p (c r t)"))
+            st["zx", i] = (xc, xsc)
+
+        def zq(i):
             cc = work.tile([P, DP, P], U32, align_bytes=64)
             csc = work.tile([P, DP, P], U8, align_bytes=64)
             nc.vector.quantize_mx(out=cc[:].rearrange("p c r -> p (c r)").bitcast(FP8X4),
                                   scales=csc[:].rearrange("p c r -> p (c r)"),
-                                  in_=cg[:].rearrange("p c r t -> p (c r t)"))
-            nc.vector.quantize_mx(out=xc[:].rearrange("p c r -> p (c r)").bitcast(FP8X4),
-                                  scales=xsc[:].rearrange("p c r -> p (c r)"),
-                                  in_=xg[:].rearrange("p c r t -> p (c r t)"))
-            st["code", i] = (xc, xsc, cc, csc)
+                                  in_=cg[i][:].rearrange("p c r t -> p (c r t)"))
+            st["zq", i] = (cc, csc)
 
-        def multiply(i):
-            xc, xsc, cc, csc = st.pop(("code", i))
-            acc = psum.tile([P, N], F32)
+        def mq(i):
+            cc, csc = st.pop(("zq", i))
+            t = psum.tile([P, N], F32, name="acc", tag="acc", bufs=ACC_BANKS)
+            acc[i] = t
             for c in range(DP):
-                nc.tensor.matmul_mx(out=acc[:], lhsT=cc[:, c, :].bitcast(FP8X4), lhsT_scale=csc[:, c, :],
+                nc.tensor.matmul_mx(out=t[:], lhsT=cc[:, c, :].bitcast(FP8X4), lhsT_scale=csc[:, c, :],
                                     rhs=rc[:, c, :].bitcast(FP8X4), rhs_scale=rsc[:, c, :],
                                     start=(c == 0), stop=False)
-            for c in range(KP):
-                nc.tensor.matmul_mx(out=acc[:], lhsT=xc[:, c, :].bitcast(FP8X4), lhsT_scale=xsc[:, c, :],
-                                    rhs=bc[:, c, :].bitcast(FP8X4), rhs_scale=bsc[:, c, :],
-                                    start=False, stop=(c == KP - 1))
-            st["acc", i] = acc
 
-        def finish(i):
-            acc = st.pop(("acc", i))
+        def mxp(i, c):
+            xc, xsc = st["zx", i]
+            nc.tensor.matmul_mx(out=acc[i][:], lhsT=xc[:, c, :].bitcast(FP8X4), lhsT_scale=xsc[:, c, :],
+                                rhs=b_code[:, c, :].bitcast(FP8X4), rhs_scale=b_scale[:, c, :],
+                                start=False, stop=(c == KP - 1))
+
+        def mx(i):
+            for c in range(KP):
+                mxp(i, c)
+
+        def m0(i):
+            mxp(i, 0)
+
+        def m1(i):
+            mxp(i, 1)
+
+        def m2(i):
+            mxp(i, 2)
+
+        def m3(i):
+            mxp(i, 3)
+
+        def fin(i):
             o = work.tile([P, N], F32, align_bytes=64)
-            nc.vector.tensor_tensor(out=o[:], in0=acc[:], in1=gbc[:], op=MULT)
+            nc.vector.tensor_tensor(out=o[:], in0=acc[i][:], in1=gbc[:], op=MULT)
             nc.sync.dma_start(out=O_v[:, i, :], in_=o[:])
 
-        for s in range(NT + 3):
-            if s >= 3:
-                finish(s - 3)
-            if 2 <= s < NT + 2:
-                quant(s - 2)
-            if s < NT:
-                widen(s)
-                add(s)
-            if s == 0:
-                for t in range(RT):
-                    r_widen(t)
-            if 1 <= s < NT + 1:
-                turn(s - 1)
-            if s == 0:
-                for t in range(RT):
-                    r_turn(t)
-                b_group(0)
-                for c in range(DP):
-                    r_quant(c)
-                b_group(1)
-                b_quant(0)
-            if s == 1:
-                b_group(2)
-                b_quant(1)
-                b_group(3)
-                b_quant(2)
-                b_quant(3)
-            if 2 <= s < NT + 2:
-                multiply(s - 2)
+        ws(0); wv(0); rw(3); rw(1); bc(0); rw(2); bc(1); rt(3); bev(0); bg(0); bev(1); rt(1); rw(0); wv(1); rt(2)
+        re(3); ad(0); rt(0); re(2); ad(1); ws(1); tx1(0); bg(2); tq(0); re(1); bg(1); eq(0); tx0(0); re(0); bz(0)
+        ex1(0); tx1(1); rz(1); ex0(0); tq(1); zq(0); ws(4); rz(0); tx0(1); zx(0); ex1(1); ad(4); mq(0); ex0(1)
+        bz(1); eq(1); wv(4); m0(0); ws(2); tx0(4); ad(2); tq(4); zx(1); tx1(4); ex0(4); zq(1); m1(0); eq(4); ad(6)
+        mq(1); ex1(4); wv(6); m0(1); ws(6); tq(6); tq(2); zq(4); bg(3); mq(4); eq(2); tx1(6); ws(5); tx0(6); zx(4)
+        tx0(2); bz(2); ex0(2); m0(4); bz(3); m1(4); eq(6); m1(1); wv(5); m2(0); ex0(6); m2(1); m2(4); wv(2); ex1(6)
+        tx1(5); ws(11); m3(1); ad(5); m3(0); m3(4); ad(3); tx0(5); ex1(5); ad(7); tq(5); ex0(5); tx1(2); fin(0)
+        tx0(11); eq(5); zq(6); tq(7); fin(1); tq(3); zq(2); eq(3); mq(6); zx(6); ex1(2); mq(2); fin(4); ws(9); m0(6)
+        zx(2); m1(6); m2(6); ad(9); m3(6); m0(2); ws(3); zq(5); m1(2); wv(3); m2(2); mq(5); fin(6); m3(2); ex0(11)
+        tx0(9); wv(9); eq(7); tx0(3); zq(3); tx1(9); ex0(3); zx(5); tx1(3); tq(9); ad(8); ex1(3); m0(5); ex0(9)
+        m1(5); zx(3); mq(3); ex1(9); ad(10); m2(5); eq(9); m3(5); ad(11); m0(3); ws(10); m1(3); wv(11); tq(8)
+        tq(11); fin(2); tq(10); eq(11); tx1(11); zq(9); tx0(10); fin(5); ex1(11); zq(11); mq(9); eq(10); zx(11)
+        mq(11); ws(7); zx(9); m2(3); m0(11); wv(10); m1(11); ex0(10); m0(9); m3(3); wv(8); eq(8); m1(9); m2(11)
+        ws(8); m2(9); wv(7); m3(9); m3(11); zq(10); tx1(10); fin(3); tx1(8); ex1(10); tx0(7); zx(10); tx1(7); tx0(8)
+        ex1(7); fin(9); mq(10); ex0(7); zq(7); zq(8); m0(10); ex0(8); fin(11); m1(10); ex1(8); m2(10); zx(7); m3(10)
+        mq(7); zx(8); mq(8); fin(10); m0(7); m1(7); m2(7); m3(7); m0(8); fin(7); m1(8); m2(8); m3(8); fin(8)

from contextlib import ExitStack

import concourse.mybir as mybir
from concourse.masks import make_identity

T, K, D, N, G = 1536, 2048, 1024, 512, 128
P = 128
NT = T // P
KP = K // 512
DP = D // 512
NB = K // G
RB = D // G
RT = N // P
S_BLOCKS = 8
TURN_BANKS = 5
WORK_BUFS = 5
S_ROWS = (0, 1)
ACC_BANKS = 3

FLOPS = 2 * T * N * (K + D)

F32 = mybir.dt.float32
BF16 = mybir.dt.bfloat16
U32 = mybir.dt.uint32
U8 = mybir.dt.uint8
FP8 = mybir.dt.float8_e4m3fn
FP8X4 = mybir.dt.float8_e4m3fn_x4
MULT = mybir.AluOpType.mult
ADD = mybir.AluOpType.add
COPY = mybir.ActivationFunctionType.Copy


def tile_relative_offset_scores_d9_kernel(tc, X_bytes, X_scale, B, Q, v, R_bytes, R_scale, g, out):
    nc = tc.nc
    with ExitStack() as ctx:
        keep = ctx.enter_context(tc.tile_pool(name="keep", bufs=1))
        work = ctx.enter_context(tc.tile_pool(name="work", bufs=WORK_BUFS))
        psum = ctx.enter_context(tc.psum_pool(name="psum", bufs=TURN_BANKS))

        vrow = keep.tile([P, D], BF16, align_bytes=64)
        nc.gpsimd.memset(vrow[:], 0.0)
        ones = keep.tile([P, P], BF16, align_bytes=64)
        nc.vector.memset(ones[:], 1.0)
        ident = keep.tile([P, P], F32, align_bytes=64)
        make_identity(nc, ident[:])

        xs = keep.tile([P, NT * NB], F32, align_bytes=64)
        rs = keep.tile([P, RT * RB], F32, align_bytes=64)
        rs32 = keep.tile([P, RT * RB], F32, align_bytes=64)
        rb = [keep.tile([P, D], U8, name=f"rb{t}", align_bytes=64) for t in range(RT)]
        xb = [keep.tile([P, K], U8, name=f"xb{i}", align_bytes=64) for i in range(NT)]
        qb = [keep.tile([P, D], BF16, name=f"qb{i}", align_bytes=64) for i in range(NT)]
        br = [keep.tile([P, 4, N], BF16, name=f"br{c}", align_bytes=64) for c in range(KP)]
        X_v = X_bytes.rearrange("(p i) k -> p i k", i=NT)
        Q_v = Q.rearrange("(p i) k -> p i k", i=NT)
        B_v = B.rearrange("(c p j) n -> c p j n", p=P, j=4)
        O_v = out.rearrange("(p i) n -> p i n", i=NT)

        def load_x(i):
            nc.sync.dma_start(out=xb[i][:], in_=X_v[:, i, :])

        def load_q(i):
            nc.sync.dma_start(out=qb[i][:], in_=Q_v[:, i, :])

        def load_r(t):
            nc.sync.dma_start(out=rb[t][:], in_=R_bytes[P * t : P * t + P, :])

        def load_b(c):
            nc.sync.dma_start(out=br[c][:], in_=B_v[c])

        nc.scalar.dma_start(out=rs[:], in_=R_scale.rearrange("a b -> (a b)").partition_broadcast(P))
        nc.scalar.dma_start(out=vrow[0:1, :], in_=v.rearrange("(o k) -> o k", o=1))
        nc.sync.dma_start(out=xs[:], in_=X_scale.rearrange("(p i) j -> p (i j)", i=NT))
        load_x(0)
        load_r(0)
        load_r(1)
        load_r(2)
        load_r(3)
        load_q(0)
        load_b(0)
        load_x(1)
        load_b(1)
        load_q(1)
        load_b(2)
        load_x(2)
        load_b(3)
        load_q(2)
        load_x(3)
        load_q(3)
        load_x(4)
        gbc = keep.tile([P, N], BF16, align_bytes=64)
        nc.sync.dma_start(out=gbc[:], in_=g.partition_broadcast(P))
        load_q(4)
        load_x(5)
        load_q(5)
        load_x(6)
        load_q(6)
        load_x(7)
        load_q(7)
        load_x(8)
        load_q(8)
        load_x(9)
        load_q(9)
        load_x(10)
        load_q(10)
        load_x(11)
        load_q(11)
        ctx.enter_context(tc.manual_schedule())

        vbc = keep.tile([P, D], BF16, align_bytes=64)
        vbc_v = vbc[:].rearrange("r (u g p e) -> r g u p e", u=2, g=DP, e=2)
        nc.vector.tensor_scalar(out=rs32[:], in0=rs[:], scalar1=1.0 / 32.0, scalar2=None, op0=MULT)
        st = {}

        def turn_bank(key):
            bank = psum.tile([P, 2, 2, P], F32, name="bank", tag="turn")
            st[key] = bank
            return bank

        def bc(h):
            bank = turn_bank(("bc", h))
            nc.tensor.matmul(bank[:].rearrange("p c u r -> p (c u r)"), lhsT=ones[:], rhs=vrow[:, 512 * h : 512 * h + 512],
                             start=True, stop=True)

        def bev(h):
            bank = st.pop(("bc", h))
            nc.scalar.copy(out=vbc_v[:, h],
                           in_=bank[:].rearrange("p c u r -> p (c u r)").rearrange("r (p u e) -> r u p e", u=2, e=2))

        rw_t = keep.tile([P, RT, D], BF16, align_bytes=64)
        rg = keep.tile([P, DP, N, 4], BF16, align_bytes=64)
        rgw = rg[:].rearrange("p c n t -> p (c n t)").bitcast(F32).rearrange("p (c n u) -> p c n u", c=DP, u=2)
        rc = keep.tile([P, DP, N], U32, align_bytes=64)
        rsc = keep.tile([P, DP, N], U8, align_bytes=64)

        def v_widen(out_tile, in_ap, scale, blk):
            c, q = blk // 4, blk % 4
            dst = out_tile.rearrange("r (c u p e) -> r c p u e", u=2, p=P, e=2)
            nc.vector.tensor_scalar(
                out=dst[:, c, 32 * q : 32 * q + 32],
                in0=in_ap[:, G * blk : G * blk + G].bitcast(FP8).rearrange("r (p u e) -> r p u e", u=2, e=2),
                scalar1=scale, scalar2=None, op0=MULT)

        def s_widen(out_tile, in_ap, scale, blk):
            nc.scalar.activation(out=out_tile[:, G * blk : G * blk + G],
                                 in_=in_ap[:, G * blk : G * blk + G].bitcast(FP8), func=COPY, scale=scale)

        def rw(t):
            for blk in range(RB):
                (s_widen if t in S_ROWS else v_widen)(
                    rw_t[:, t, :], rb[t][:], rs32[:, RB * t + blk : RB * t + blk + 1], blk)

        def transposes(bank, words, first, natural):
            for c in range(2):
                for u in range(2):
                    w = 256 * (first + c)
                    src = words[:, w + u : w + 256 : 2] if natural else words[:, w + P * u : w + P * u + P]
                    nc.tensor.transpose(bank[:, c, u, :], src, ident[:])

        def rt(t):
            transposes(turn_bank(("rt", t)), rw_t[:, t, :].bitcast(F32), 0, t in S_ROWS)

        def re(t):
            bank = st.pop(("rt", t))
            nc.scalar.copy(out=rgw[:, :, P * t : P * t + P, :], in_=bank[:].rearrange("p c u r -> p c r u"))

        def rz(c):
            nc.vector.quantize_mx(out=rc[:, c, :].bitcast(FP8X4), scales=rsc[:, c, :],
                                  in_=rg[:, c].rearrange("p n t -> p (n t)"))

        b_grp = [keep.tile([P, N, 4], BF16, name=f"bg{c}", align_bytes=64) for c in range(KP)]
        b_code = keep.tile([P, KP, N], U32, align_bytes=64)
        b_scale = keep.tile([P, KP, N], U8, align_bytes=64)

        def bg(c):
            nc.vector.tensor_copy(out=b_grp[c][:], in_=br[c][:].rearrange("p j n -> p n j"))

        def bz(c):
            nc.vector.quantize_mx(out=b_code[:, c, :].bitcast(FP8X4), scales=b_scale[:, c, :],
                                  in_=b_grp[c][:].rearrange("p n t -> p (n t)"))

        xw = [None] * NT
        cw = [None] * NT
        xg = [None] * NT
        cg = [None] * NT
        codes = [None] * NT
        acc = [None] * NT

        def xw_tile(i):
            if xw[i] is None:
                t = work.tile([P, K], BF16, name="xw", align_bytes=64)
                xw[i] = t

        def ws(i):
            xw_tile(i)
            for blk in range(S_BLOCKS):
                s_widen(xw[i][:], xb[i][:], xs[:, NB * i + blk : NB * i + blk + 1], blk)

        def wv(i):
            xw_tile(i)
            for blk in range(S_BLOCKS, NB):
                v_widen(xw[i][:], xb[i][:], xs[:, NB * i + blk : NB * i + blk + 1], blk)

        def ad(i):
            t = work.tile([P, D], BF16, name="cw", align_bytes=64)
            cw[i] = t
            nc.vector.tensor_tensor(
                out=t[:].rearrange("r (u w e) -> r u w e", u=2, e=2),
                in0=qb[i][:].rearrange("r (w u e) -> r u w e", u=2, e=2),
                in1=vbc[:].rearrange("r (u w e) -> r u w e", u=2, e=2), op=ADD)

        def tx0(i):
            transposes(turn_bank(("x0", i)), xw[i][:].bitcast(F32), 0, S_BLOCKS >= 8)

        def tx1(i):
            transposes(turn_bank(("x1", i)), xw[i][:].bitcast(F32), 2, False)

        def xg_words(i):
            if xg[i] is None:
                t = work.tile([P, KP, P, 4], BF16, name="xg", align_bytes=64)
                xg[i] = t
            return xg[i][:].rearrange("p c r t -> p (c r t)").bitcast(F32).rearrange("p (c r u) -> p c r u", c=KP, u=2)

        def ex0(i):
            bank = st.pop(("x0", i))
            nc.scalar.copy(out=xg_words(i)[:, 0:2], in_=bank[:].rearrange("p c u r -> p c r u"))

        def ex1(i):
            bank = st.pop(("x1", i))
            nc.scalar.copy(out=xg_words(i)[:, 2:4], in_=bank[:].rearrange("p c u r -> p c r u"))

        def tq(i):
            bank = turn_bank(("q", i))
            words = cw[i][:].bitcast(F32)
            for c in range(DP):
                for u in range(2):
                    w = 256 * u + P * c
                    nc.tensor.transpose(bank[:, c, u, :], words[:, w : w + P], ident[:])

        def eq(i):
            bank = st.pop(("q", i))
            t = work.tile([P, DP, P, 4], BF16, name="cg", align_bytes=64)
            cg[i] = t
            words = t[:].rearrange("p c r t -> p (c r t)").bitcast(F32).rearrange("p (c r u) -> p c r u", c=DP, u=2)
            nc.scalar.copy(out=words, in_=bank[:].rearrange("p c u r -> p c r u"))

        def zx(i):
            xc = work.tile([P, KP, P], U32, align_bytes=64)
            xsc = work.tile([P, KP, P], U8, align_bytes=64)
            nc.vector.quantize_mx(out=xc[:].rearrange("p c r -> p (c r)").bitcast(FP8X4),
                                  scales=xsc[:].rearrange("p c r -> p (c r)"),
                                  in_=xg[i][:].rearrange("p c r t -> p (c r t)"))
            st["zx", i] = (xc, xsc)

        def zq(i):
            cc = work.tile([P, DP, P], U32, align_bytes=64)
            csc = work.tile([P, DP, P], U8, align_bytes=64)
            nc.vector.quantize_mx(out=cc[:].rearrange("p c r -> p (c r)").bitcast(FP8X4),
                                  scales=csc[:].rearrange("p c r -> p (c r)"),
                                  in_=cg[i][:].rearrange("p c r t -> p (c r t)"))
            st["zq", i] = (cc, csc)

        def mq(i):
            cc, csc = st.pop(("zq", i))
            t = psum.tile([P, N], F32, name="acc", tag="acc", bufs=ACC_BANKS)
            acc[i] = t
            for c in range(DP):
                nc.tensor.matmul_mx(out=t[:], lhsT=cc[:, c, :].bitcast(FP8X4), lhsT_scale=csc[:, c, :],
                                    rhs=rc[:, c, :].bitcast(FP8X4), rhs_scale=rsc[:, c, :],
                                    start=(c == 0), stop=False)

        def mxp(i, c):
            xc, xsc = st["zx", i]
            nc.tensor.matmul_mx(out=acc[i][:], lhsT=xc[:, c, :].bitcast(FP8X4), lhsT_scale=xsc[:, c, :],
                                rhs=b_code[:, c, :].bitcast(FP8X4), rhs_scale=b_scale[:, c, :],
                                start=False, stop=(c == KP - 1))

        def mx(i):
            for c in range(KP):
                mxp(i, c)

        def m0(i):
            mxp(i, 0)

        def m1(i):
            mxp(i, 1)

        def m2(i):
            mxp(i, 2)

        def m3(i):
            mxp(i, 3)

        def fin(i):
            o = work.tile([P, N], F32, align_bytes=64)
            nc.vector.tensor_tensor(out=o[:], in0=acc[i][:], in1=gbc[:], op=MULT)
            nc.sync.dma_start(out=O_v[:, i, :], in_=o[:])

        ws(0); wv(0); rw(3); rw(1); bc(0); rw(2); bc(1); rt(3); bev(0); bg(0); bev(1); rt(1); rw(0); wv(1); rt(2)
        re(3); ad(0); rt(0); re(2); ad(1); ws(1); tx1(0); bg(2); tq(0); re(1); bg(1); eq(0); tx0(0); re(0); bz(0)
        ex1(0); tx1(1); rz(1); ex0(0); tq(1); zq(0); ws(4); rz(0); tx0(1); zx(0); ex1(1); ad(4); mq(0); ex0(1)
        bz(1); eq(1); wv(4); m0(0); ws(2); tx0(4); ad(2); tq(4); zx(1); tx1(4); ex0(4); zq(1); m1(0); eq(4); ad(6)
        mq(1); ex1(4); wv(6); m0(1); ws(6); tq(6); tq(2); zq(4); bg(3); mq(4); eq(2); tx1(6); ws(5); tx0(6); zx(4)
        tx0(2); bz(2); ex0(2); m0(4); bz(3); m1(4); eq(6); m1(1); wv(5); m2(0); ex0(6); m2(1); m2(4); wv(2); ex1(6)
        tx1(5); ws(11); m3(1); ad(5); m3(0); m3(4); ad(3); tx0(5); ex1(5); ad(7); tq(5); ex0(5); tx1(2); fin(0)
        tx0(11); eq(5); zq(6); tq(7); fin(1); tq(3); zq(2); eq(3); mq(6); zx(6); ex1(2); mq(2); fin(4); ws(9); m0(6)
        zx(2); m1(6); m2(6); ad(9); m3(6); m0(2); ws(3); zq(5); m1(2); wv(3); m2(2); mq(5); fin(6); m3(2); ex0(11)
        tx0(9); wv(9); eq(7); tx0(3); zq(3); tx1(9); ex0(3); zx(5); tx1(3); tq(9); ad(8); ex1(3); m0(5); ex0(9)
        m1(5); zx(3); mq(3); ex1(9); ad(10); m2(5); eq(9); m3(5); ad(11); m0(3); ws(10); m1(3); wv(11); tq(8)
        tq(11); fin(2); tq(10); eq(11); tx1(11); zq(9); tx0(10); fin(5); ex1(11); zq(11); mq(9); eq(10); zx(11)
        mq(11); ws(7); zx(9); m2(3); m0(11); wv(10); m1(11); ex0(10); m0(9); m3(3); wv(8); eq(8); m1(9); m2(11)
        ws(8); m2(9); wv(7); m3(9); m3(11); zq(10); tx1(10); fin(3); tx1(8); ex1(10); tx0(7); zx(10); tx1(7); tx0(8)
        ex1(7); fin(9); mq(10); ex0(7); zq(7); zq(8); m0(10); ex0(8); fin(11); m1(10); ex1(8); m2(10); zx(7); m3(10)
        mq(7); zx(8); mq(8); fin(10); m0(7); m1(7); m2(7); m3(7); m0(8); fin(7); m1(8); m2(8); m3(8); fin(8)
